import numpy as np
import ml_dtypes


def mxq(x, axis, fmt="e4m3"):
    dtype, down = {"e4m3": (ml_dtypes.float8_e4m3fn, 7), "e5m2": (ml_dtypes.float8_e5m2, 14)}[fmt]
    v = np.moveaxis(np.asarray(x, np.float32).astype(ml_dtypes.bfloat16).astype(np.float64), axis, -1)
    blocks = v.reshape(v.shape[:-1] + (-1, 32))
    amax = np.abs(blocks).max(-1, keepdims=True)
    byte = np.maximum(np.where(amax > 0, np.frexp(amax)[1] - 1 + 127, 0) - down, 1)
    scale = np.exp2(byte - 127.0)
    codes = (blocks / scale).astype(np.float32).astype(dtype).astype(np.float64)
    return np.moveaxis((codes * scale).reshape(v.shape), -1, axis)


WIDE = False


def mx_kscale(k):
    if not WIDE:
        return np.ones(k)
    levels = np.array([10, -10, 5, -5, 0])
    if k % 512:
        return np.exp2(np.random.permutation(np.resize(levels, k // 32))).repeat(32)
    a = np.empty((k // 512, 16))
    for p in range(k // 512):
        a[p, :8] = np.random.permutation(np.resize(levels, 8))
        for g in range(8):
            far = levels[np.abs(levels - a[p, g]) >= 10]
            a[p, g + 8] = far[np.random.randint(len(far))]
    return np.exp2(a.ravel()).repeat(32)


def f64(x):
    return np.asarray(x).astype(np.float64)


def striped(idx):
    return np.tile(np.asarray(idx).reshape(-1, 16).T, (8, 1)).astype(np.uint16)


def unstriped(offs):
    return offs[:16].T.reshape(-1).astype(np.int64)


E2M1 = np.array([0.0, 0.5, 1.0, 1.5, 2.0, 3.0, 4.0, 6.0, -0.0, -0.5, -1.0, -1.5, -2.0, -3.0, -4.0, -6.0])


def pack_weight(w, fmt):
    k, n = w.shape
    w = f64(np.asarray(w, np.float32).astype(ml_dtypes.bfloat16)).reshape(k // 32, 32, n)
    amax = np.abs(w).max(1)
    if fmt == "e4m3":
        byte = np.frexp(amax)[1] - 1 + 127 - 7
    else:
        mant, ex = np.frexp(amax / 6.0)
        byte = np.where(mant > 0.5, ex, ex - 1) + 127
    byte = np.clip(np.where(amax > 0, byte, 1), 1, 254)
    scaled = (w * np.exp2(127.0 - byte)[:, None, :]).reshape(k, n).astype(np.float32)
    by_word = np.ascontiguousarray(scaled.reshape(k // 512, 128, 4, n).transpose(0, 1, 3, 2))
    if fmt == "e4m3":
        words = by_word.astype(ml_dtypes.float8_e4m3fn).view(np.uint8)
    else:
        c = by_word.astype(ml_dtypes.float4_e2m1fn).view(np.uint8) & 0xF
        words = (c[..., 0::2] | (c[..., 1::2] << 4)).reshape(k // 512, 128, 2 * n)
    return np.ascontiguousarray(words), np.ascontiguousarray(byte.astype(np.uint8).reshape(k // 512, 16, n))


def unpack_weight(words, scales, fmt):
    g, _, n = scales.shape
    words = np.ascontiguousarray(words).reshape(g, 128, n, -1)
    if fmt == "e4m3":
        vals = words.view(ml_dtypes.float8_e4m3fn).astype(np.float64)
    else:
        nib = np.empty((g, 128, n, 4), np.uint8)
        nib[..., 0::2] = words & 0xF
        nib[..., 1::2] = words >> 4
        vals = E2M1[nib]
    vals = vals * np.repeat(np.exp2(scales.astype(np.float64) - 127.0), 8, axis=1)[..., None]
    return vals.transpose(0, 1, 3, 2).reshape(g * 512, n)


D, T, I, M = 512, 2048, 512, 512


def setup_inputs():
    n = np.random.standard_normal
    idx = np.random.permutation(T)[:I]
    fd = mx_kscale(D)
    ptsp = pack_weight(n((D, T)) / fd[:, None], "e2m1")
    return {
        "pts_words": ptsp[0],
        "pts_scales": ptsp[1],
        "cent": (n((D, M)) * 0.2 / np.sqrt(D) * fd[:, None]).astype(np.float32),
        "pn": (np.random.uniform(1.0, 2.0, (I, 1))).astype(np.float32),
        "cn": (np.random.uniform(1.0, 2.0, (1, M))).astype(np.float32),
        "offs": striped(idx),
    }


def reference(pts_words, pts_scales, cent, pn, cn, offs):
    idx = unstriped(offs)
    ptsu = unpack_weight(pts_words, pts_scales, "e2m1")
    ptsidxg = ptsu[:, idx]
    centq = mxq(f64(cent), 0, "e4m3")
    a = ptsidxg.T @ centq
    r = 1.0 / (1.0 + f64(pn) + f64(cn) - 2.0 * a)
    s = r / np.sum(r, axis=1, keepdims=True)
    st = s.T
    x = np.square(st) / np.sum(st, axis=1, keepdims=True)
    xt = x.T
    y = xt / np.sum(xt, axis=1, keepdims=True) * 512.0
    return y

@@ -1,0 +1,242 @@
+from contextlib import ExitStack
+
+import concourse.mybir as mybir
+
+D, T, I, M = 512, 2048, 512, 512
+FLOPS = 2 * D * I * M
+
+F32 = mybir.dt.float32
+BF16 = mybir.dt.bfloat16
+I32 = mybir.dt.int32
+U32 = mybir.dt.uint32
+U16 = mybir.dt.uint16
+U8 = mybir.dt.uint8
+FP8X4 = mybir.dt.float8_e4m3fn_x4
+FP4X4 = mybir.dt.float4_e2m1fn_x4
+ALU = mybir.AluOpType
+ACT = mybir.ActivationFunctionType
+AX = mybir.AxisListType
+
+P = 128
+PACK = 4
+TILES = I // P
+BLOCKS = M // P
+HALF = M // 2
+
+
+def tile_attend_dectarget_kernel(tc, pts_words, pts_scales, cent, pn, cn, offs, out):
+    nc = tc.nc
+    with ExitStack() as ctx:
+        sb = ctx.enter_context(tc.tile_pool(name="sb", bufs=1))
+        ps = ctx.enter_context(tc.psum_pool(name="ps", bufs=1))
+
+        offsets = sb.tile([P, I // 16], U16, name="offsets")
+        words = sb.tile([P, T], U16, name="words", align_bytes=64)
+        plane = sb.tile([P, T], U8, name="plane", align_bytes=64)
+        raw = [sb.tile([P, PACK, HALF], F32, name="raw%d" % h) for h in range(2)]
+        pn_col = sb.tile([P, TILES], F32, name="pn_col")
+        cn_col = sb.tile([P, BLOCKS], F32, name="cn_col")
+        ident = sb.tile([P, P], F32, name="ident")
+
+        nc.vector.memset(plane[:].bitcast(I32), 0)
+        ones = sb.tile([P, 32], F32, name="ones")
+        ramp = sb.tile([P, 32], F32, name="ramp", align_bytes=64)
+        lane = sb.tile([P, 32], F32, name="lane", align_bytes=64)
+        nc.vector.memset(ones[:], 1.0)
+        nc.vector.memset(ident[:], 0.0)
+        nc.vector.tensor_tensor_scan(ramp[:], ones[:], ones[:], -1.0, ALU.mult, ALU.add)
+        nc.vector.transpose(lane[:], ramp[:])
+        for c in range(4):
+            rows = slice(32 * c, 32 * c + 32)
+            nc.vector.tensor_tensor(ident[rows, rows], ramp[rows, :], lane[rows, :], ALU.is_equal)
+
+        cent_rows = cent.rearrange("(p j) m -> p j m", j=PACK)
+        nc.sync.dma_start(offsets[:], offs)
+        nc.sync.dma_start(raw[0][:], cent_rows[:, :, 0:HALF])
+        nc.sync.dma_start(cn_col[:], cn.rearrange("o (p b) -> p (o b)", p=P))
+        for q in range(4):
+            nc.sync.dma_start(
+                plane[32 * q : 32 * q + 4, :].bitcast(I32),
+                pts_scales[0, 4 * q : 4 * q + 4, :].bitcast(I32),
+            )
+        nc.sync.dma_start(words[:].bitcast(I32), pts_words[0].bitcast(I32))
+        with nc.allow_non_contiguous_dma(reason="one number a partition"):
+            nc.sync.dma_start(pn_col[:], pn.rearrange("(t p) o -> p (t o)", p=P))
+        nc.sync.dma_start(raw[1][:], cent_rows[:, :, HALF:M])
+
+        row_ps = ps.tile([P, M], F32, name="row_ps")
+        for b in range(BLOCKS):
+            nc.tensor.transpose(row_ps[:, b * P : (b + 1) * P], cn_col[:, b : b + 1].to_broadcast([P, P]), ident[:])
+        cn1 = sb.tile([P, M], F32, name="cn1")
+
+        cscale = [sb.tile([P, HALF], U8, name="cscale%d" % h, align_bytes=64) for h in range(2)]
+        gw = [sb.tile([P, I // 2], U16, name="gw%d" % h, align_bytes=64) for h in range(2)]
+        gs = sb.tile([P, I], U8, name="gs", align_bytes=64)
+        grouped = [sb.tile([P, HALF, PACK], BF16, name="grouped%d" % h, align_bytes=64) for h in range(2)]
+
+        def cast(h):
+            nc.scalar.activation(
+                out=grouped[h][:], in_=raw[h][:].rearrange("p j w -> p w j"), func=ACT.Copy, scale=-2.0
+            )
+
+        def quant(h):
+            nc.vector.quantize_mx(
+                out=codes[h][:].bitcast(FP8X4),
+                scales=cscale[h][:],
+                in_=grouped[h][:].rearrange("p w j -> p (w j)"),
+            )
+
+        def paired(name):
+            return [sb.tile([P, 2, 2, HALF], F32, name="%s%d" % (name, c)) for c in range(2)]
+
+        def wide(name):
+            return [sb.tile([P, M], F32, name="%s%d" % (name, t)) for t in range(TILES)]
+
+        def narrow(name):
+            return [sb.tile([P, 1], F32, name="%s%d" % (name, t)) for t in range(TILES)]
+
+        x, u, v, g = [paired(n) for n in ("x", "u", "v", "g")]
+        q, r, s, y, res = [wide(n) for n in ("q", "r", "s", "y", "res")]
+        rs, ir, ys, iy, k = [narrow(n) for n in ("rs", "ir", "ys", "iy", "k")]
+        colsum = []
+
+        def score(tiles, h):
+            name = "row_ps" if (tiles[0], h) == (0, 0) else "a_ps%d%d" % (tiles[0], h)
+            a_ps = ps.tile([P, 2, HALF], F32, name=name)
+            for e, t in enumerate(tiles):
+                nc.tensor.matmul_mx(
+                    out=a_ps[:, e, :],
+                    lhsT=gw[t // 2][:, (t % 2) * P : (t % 2 + 1) * P].bitcast(FP4X4),
+                    lhsT_scale=gs[:, t * P : (t + 1) * P],
+                    rhs=codes[h][:].bitcast(FP8X4),
+                    rhs_scale=cscale[h][:],
+                    start=True,
+                    stop=True,
+                )
+            for e, t in enumerate(tiles):
+                nc.vector.scalar_tensor_tensor(
+                    out=x[t // 2][:, h, t % 2, :],
+                    in0=a_ps[:, e, :],
+                    scalar=pn_col[:, t : t + 1],
+                    in1=cn1[:, h * HALF : (h + 1) * HALF],
+                    op0=ALU.add,
+                    op1=ALU.add,
+                )
+
+        def part(arr, tiles, h):
+            c = tiles[0] // 2
+            return arr[c][:, h, tiles[0] % 2 : tiles[-1] % 2 + 1, :]
+
+        def root(tiles, h):
+            nc.scalar.activation(out=part(u, tiles, h), in_=part(x, tiles, h), func=ACT.Abs_reciprocal_sqrt)
+
+        def square(tiles, h):
+            nc.scalar.activation(out=part(v, tiles, h), in_=part(u, tiles, h), func=ACT.Square)
+
+        def sign(tiles, h):
+            nc.vector.tensor_scalar(
+                out=part(g, tiles, h), in0=part(x, tiles, h), scalar1=0.0, scalar2=0.5, op0=ALU.is_ge, op1=ALU.subtract
+            )
+
+        def recip(t):
+            nc.vector.scalar_tensor_tensor(
+                out=r[t][:].rearrange("p (h w) -> p h w", h=2),
+                in0=g[t // 2][:, :, t % 2, :],
+                scalar=1.0,
+                in1=v[t // 2][:, :, t % 2, :],
+                op0=ALU.mult,
+                op1=ALU.mult,
+                accum_out=rs[t][:],
+            )
+            nc.vector.reciprocal(ir[t][:], rs[t][:])
+
+        def assign(t, on_vector, halves):
+            for h in range(halves):
+                cols = slice(h * M // halves, (h + 1) * M // halves)
+                if on_vector:
+                    nc.vector.tensor_scalar(out=s[t][:, cols], in0=r[t][:, cols], scalar1=ir[t][:], scalar2=None, op0=ALU.mult)
+                else:
+                    nc.scalar.activation(out=s[t][:, cols], in_=r[t][:, cols], func=ACT.Copy, scale=ir[t][:])
+            for b in range(BLOCKS):
+                if t == 0:
+                    colsum.append(ps.tile([P, P], F32, name=("a_ps10", "a_ps20", "sum2", "sum3")[b]))
+                nc.tensor.matmul(
+                    colsum[b][:],
+                    lhsT=s[t][:, b * P : (b + 1) * P],
+                    rhs=ident[:],
+                    is_transpose=True,
+                    start=(t == 0),
+                    stop=(t == TILES - 1),
+                )
+
+        cast(0)
+        nc.scalar.activation(
+            out=cn1[:].rearrange("p (n b) -> p n b", b=BLOCKS),
+            in_=row_ps[:].rearrange("p (b n) -> p n b", b=BLOCKS),
+            func=ACT.Copy,
+            bias=1.0,
+        )
+        cast(1)
+        nc.vector.tensor_copy(gs[:], plane[:].indirect(offsets[:]))
+        codes = [sb.tile([P, HALF], U32, name=n, align_bytes=64) for n in ("plane", "codes1")]
+        quant(0)
+        for h in range(2):
+            nc.vector.tensor_copy(gw[h][:], words[:].indirect(offsets[:, 16 * h : 16 * h + 16]))
+        score((0,), 0)
+        score((1,), 0)
+        quant(1)
+        score((0,), 1)
+        score((1,), 1)
+        score((2, 3), 0)
+        score((2, 3), 1)
+        root((0, 1), 0)
+        square((0, 1), 0)
+        root((0,), 1)
+        square((0,), 1)
+        root((1,), 1)
+        square((1,), 1)
+        root((2, 3), 0)
+        square((2, 3), 0)
+        root((2,), 1)
+        square((2,), 1)
+        root((3,), 1)
+        square((3,), 1)
+        sign((0, 1), 0)
+        sign((0, 1), 1)
+        recip(0)
+        recip(1)
+        sign((2, 3), 0)
+        sign((2, 3), 1)
+        recip(2)
+        assign(0, False, 1)
+        assign(1, True, 1)
+        recip(3)
+        assign(2, False, 1)
+        assign(3, True, 2)
+        for t in range(TILES):
+            nc.scalar.activation(out=q[t][:], in_=r[t][:], func=ACT.Square, scale=ir[t][:])
+
+        w_ps = ps.tile([P, M], F32, name="row_ps")
+        for b in range(BLOCKS):
+            ssum = sb.tile([P, 1], F32, name="ssum%d" % b)
+            nc.vector.tensor_reduce(out=ssum[:], in_=colsum[b][:], axis=AX.X, op=ALU.add)
+            w = sb.tile([P, 1], F32, name="w%d" % b)
+            nc.vector.reciprocal(w[:], ssum[:])
+            nc.tensor.transpose(w_ps[:, b * P : (b + 1) * P], w[:].to_broadcast([P, P]), ident[:])
+
+        for t in range(TILES):
+            nc.vector.scalar_tensor_tensor(
+                out=y[t][:], in0=q[t][:], scalar=1.0, in1=w_ps[:], op0=ALU.mult, op1=ALU.mult, accum_out=ys[t][:]
+            )
+            nc.vector.reciprocal(iy[t][:], ys[t][:])
+            if t < TILES - 1:
+                nc.gpsimd.tensor_scalar(out=k[t][:], in0=iy[t][:], scalar1=512.0, scalar2=1.0, op0=ALU.mult, op1=ALU.mult)
+            for h in range(1):
+                cols = slice(h * M // 1, (h + 1) * M // 1)
+                if t == TILES - 1:
+                    nc.vector.tensor_scalar(
+                        out=res[t][:, cols], in0=y[t][:, cols], scalar1=iy[t][:], scalar2=512.0, op0=ALU.mult, op1=ALU.mult
+                    )
+                else:
+                    nc.scalar.activation(out=res[t][:, cols], in_=y[t][:, cols], func=ACT.Copy, scale=k[t][:])
+                nc.sync.dma_start(out[t * P : (t + 1) * P, cols], res[t][:, cols])

@@ -49,6 +49,8 @@ def tile_attend_dectarget_kernel(tc, pts_words, pts_scales, cent, pn, cn, offs, 
         for c in range(4):
             rows = slice(32 * c, 32 * c + 32)
             nc.vector.tensor_tensor(ident[rows, rows], ramp[rows, :], lane[rows, :], ALU.is_equal)
+        warm = sb.tile([P, 1], F32, name="warm")
+        nc.scalar.activation(out=warm[:], in_=ones[:, 0:1], func=ACT.Abs_reciprocal_sqrt)
 
         cent_rows = cent.rearrange("(p j) m -> p j m", j=PACK)
         nc.sync.dma_start(offsets[:], offs)

@@ -22,6 +22,7 @@ PACK = 4
 TILES = I // P
 BLOCKS = M // P
 HALF = M // 2
+TINY = 2.0**-60
 
 
 def tile_attend_dectarget_kernel(tc, pts_words, pts_scales, cent, pn, cn, offs, out):
@@ -62,9 +63,9 @@ def tile_attend_dectarget_kernel(tc, pts_words, pts_scales, cent, pn, cn, offs, 
                 pts_scales[0, 4 * q : 4 * q + 4, :].bitcast(I32),
             )
         nc.sync.dma_start(words[:].bitcast(I32), pts_words[0].bitcast(I32))
-        with nc.allow_non_contiguous_dma(reason="one number a partition"):
-            nc.sync.dma_start(pn_col[:], pn.rearrange("(t p) o -> p (t o)", p=P))
         nc.sync.dma_start(raw[1][:], cent_rows[:, :, HALF:M])
+        with nc.allow_non_contiguous_dma(reason="one number a partition"):
+            nc.gpsimd.dma_start(pn_col[:], pn.rearrange("(t p) o -> p (t o)", p=P))
 
         row_ps = ps.tile([P, M], F32, name="row_ps")
         for b in range(BLOCKS):
@@ -72,13 +73,15 @@ def tile_attend_dectarget_kernel(tc, pts_words, pts_scales, cent, pn, cn, offs, 
         cn1 = sb.tile([P, M], F32, name="cn1")
 
         cscale = [sb.tile([P, HALF], U8, name="cscale%d" % h, align_bytes=64) for h in range(2)]
-        gw = [sb.tile([P, I // 2], U16, name="gw%d" % h, align_bytes=64) for h in range(2)]
         gs = sb.tile([P, I], U8, name="gs", align_bytes=64)
         grouped = [sb.tile([P, HALF, PACK], BF16, name="grouped%d" % h, align_bytes=64) for h in range(2)]
 
         def cast(h):
             nc.scalar.activation(
-                out=grouped[h][:], in_=raw[h][:].rearrange("p j w -> p w j"), func=ACT.Copy, scale=-2.0
+                out=grouped[h][:].rearrange("p (c i) j -> p c j i", i=4),
+                in_=raw[h][:].rearrange("p j (c i) -> p c j i", i=4),
+                func=ACT.Copy,
+                scale=-2.0,
             )
 
         def quant(h):
@@ -136,8 +139,9 @@ def tile_attend_dectarget_kernel(tc, pts_words, pts_scales, cent, pn, cn, offs, 
             nc.scalar.activation(out=part(v, tiles, h), in_=part(u, tiles, h), func=ACT.Square)
 
         def sign(tiles, h):
-            nc.vector.tensor_scalar(
-                out=part(g, tiles, h), in0=part(x, tiles, h), scalar1=0.0, scalar2=0.5, op0=ALU.is_ge, op1=ALU.subtract
+            engine = nc.gpsimd if h == 0 else nc.vector
+            engine.tensor_scalar(
+                out=part(g, tiles, h), in0=part(x, tiles, h), scalar1=TINY, scalar2=-TINY, op0=ALU.min, op1=ALU.max
             )
 
         def recip(t):
@@ -182,6 +186,7 @@ def tile_attend_dectarget_kernel(tc, pts_words, pts_scales, cent, pn, cn, offs, 
         nc.vector.tensor_copy(gs[:], plane[:].indirect(offsets[:]))
         codes = [sb.tile([P, HALF], U32, name=n, align_bytes=64) for n in ("plane", "codes1")]
         quant(0)
+        gw = [sb.tile([P, I // 2], U16, name=n, align_bytes=64) for n in ("gw0", "gw1")]
         for h in range(2):
             nc.vector.tensor_copy(gw[h][:], words[:].indirect(offsets[:, 16 * h : 16 * h + 16]))
         score((0,), 0)
@@ -191,8 +196,10 @@ def tile_attend_dectarget_kernel(tc, pts_words, pts_scales, cent, pn, cn, offs, 
         score((1,), 1)
         score((2, 3), 0)
         score((2, 3), 1)
-        root((0, 1), 0)
-        square((0, 1), 0)
+        root((0,), 0)
+        root((1,), 0)
+        square((0,), 0)
+        square((1,), 0)
         root((0,), 1)
         square((0,), 1)
         root((1,), 1)
@@ -208,9 +215,9 @@ def tile_attend_dectarget_kernel(tc, pts_words, pts_scales, cent, pn, cn, offs, 
         recip(0)
         recip(1)
         sign((2, 3), 0)
+        assign(0, True, 1)
         sign((2, 3), 1)
         recip(2)
-        assign(0, False, 1)
         assign(1, True, 1)
         recip(3)
         assign(2, False, 1)
@@ -231,11 +238,11 @@ def tile_attend_dectarget_kernel(tc, pts_words, pts_scales, cent, pn, cn, offs, 
                 out=y[t][:], in0=q[t][:], scalar=1.0, in1=w_ps[:], op0=ALU.mult, op1=ALU.mult, accum_out=ys[t][:]
             )
             nc.vector.reciprocal(iy[t][:], ys[t][:])
-            if t < TILES - 1:
-                nc.gpsimd.tensor_scalar(out=k[t][:], in0=iy[t][:], scalar1=512.0, scalar2=1.0, op0=ALU.mult, op1=ALU.mult)
+            if t == 0:
+                nc.scalar.activation(out=k[t][:], in_=iy[t][:], func=ACT.Copy, scale=512.0)
             for h in range(1):
                 cols = slice(h * M // 1, (h + 1) * M // 1)
-                if t == TILES - 1:
+                if t > 0:
                     nc.vector.tensor_scalar(
                         out=res[t][:, cols], in0=y[t][:, cols], scalar1=iy[t][:], scalar2=512.0, op0=ALU.mult, op1=ALU.mult
                     )

@@ -22,6 +22,7 @@ PACK = 4
 TILES = I // P
 BLOCKS = M // P
 HALF = M // 2
+SPLIT = 192
 TINY = 2.0**-60
 
 
@@ -76,13 +77,13 @@ def tile_attend_dectarget_kernel(tc, pts_words, pts_scales, cent, pn, cn, offs, 
         gs = sb.tile([P, I], U8, name="gs", align_bytes=64)
         grouped = [sb.tile([P, HALF, PACK], BF16, name="grouped%d" % h, align_bytes=64) for h in range(2)]
 
-        def cast(h):
-            nc.scalar.activation(
-                out=grouped[h][:].rearrange("p (c i) j -> p c j i", i=4),
-                in_=raw[h][:].rearrange("p j (c i) -> p c j i", i=4),
-                func=ACT.Copy,
-                scale=-2.0,
-            )
+        def cast(h, lo, hi, on_vector):
+            dst = grouped[h][:, lo:hi, :].rearrange("p (c i) j -> p c j i", i=4)
+            src = raw[h][:, :, lo:hi].rearrange("p j (c i) -> p c j i", i=4)
+            if on_vector:
+                nc.vector.tensor_scalar(out=dst, in0=src, scalar1=-2.0, scalar2=None, op0=ALU.mult)
+            else:
+                nc.scalar.activation(out=dst, in_=src, func=ACT.Copy, scale=-2.0)
 
         def quant(h):
             nc.vector.quantize_mx(
@@ -100,7 +101,8 @@ def tile_attend_dectarget_kernel(tc, pts_words, pts_scales, cent, pn, cn, offs, 
         def narrow(name):
             return [sb.tile([P, 1], F32, name="%s%d" % (name, t)) for t in range(TILES)]
 
-        x, u, v, g = [paired(n) for n in ("x", "u", "v", "g")]
+        u, v, g = [paired(n) for n in ("u", "v", "g")]
+        x = []
         q, r, s, y, res = [wide(n) for n in ("q", "r", "s", "y", "res")]
         rs, ir, ys, iy, k = [narrow(n) for n in ("rs", "ir", "ys", "iy", "k")]
         colsum = []
@@ -131,6 +133,9 @@ def tile_attend_dectarget_kernel(tc, pts_words, pts_scales, cent, pn, cn, offs, 
         def part(arr, tiles, h):
             c = tiles[0] // 2
             return arr[c][:, h, tiles[0] % 2 : tiles[-1] % 2 + 1, :]
+
+        def square_v(tiles, h):
+            nc.vector.tensor_tensor(part(v, tiles, h), part(u, tiles, h), part(u, tiles, h), ALU.mult)
 
         def root(tiles, h):
             nc.scalar.activation(out=part(u, tiles, h), in_=part(x, tiles, h), func=ACT.Abs_reciprocal_sqrt)
@@ -175,49 +180,51 @@ def tile_attend_dectarget_kernel(tc, pts_words, pts_scales, cent, pn, cn, offs, 
                     stop=(t == TILES - 1),
                 )
 
-        cast(0)
+        cast(0, 0, HALF, False)
         nc.scalar.activation(
             out=cn1[:].rearrange("p (n b) -> p n b", b=BLOCKS),
             in_=row_ps[:].rearrange("p (b n) -> p n b", b=BLOCKS),
             func=ACT.Copy,
             bias=1.0,
         )
-        cast(1)
+        cast(1, 0, SPLIT, False)
         nc.vector.tensor_copy(gs[:], plane[:].indirect(offsets[:]))
         codes = [sb.tile([P, HALF], U32, name=n, align_bytes=64) for n in ("plane", "codes1")]
         quant(0)
         gw = [sb.tile([P, I // 2], U16, name=n, align_bytes=64) for n in ("gw0", "gw1")]
         for h in range(2):
             nc.vector.tensor_copy(gw[h][:], words[:].indirect(offsets[:, 16 * h : 16 * h + 16]))
+        cast(1, SPLIT, HALF, True)
+        quant(1)
+        x_all = sb.tile([P, 2, 2, 2, HALF], F32, name="grouped1", align_bytes=64)
+        x.extend([x_all[:, 0], x_all[:, 1]])
         score((0,), 0)
         score((1,), 0)
-        quant(1)
+        score((2, 3), 0)
         score((0,), 1)
         score((1,), 1)
-        score((2, 3), 0)
         score((2, 3), 1)
-        root((0,), 0)
-        root((1,), 0)
-        square((0,), 0)
-        square((1,), 0)
-        root((0,), 1)
-        square((0,), 1)
-        root((1,), 1)
-        square((1,), 1)
+        root((0, 1), 0)
         root((2, 3), 0)
-        square((2, 3), 0)
+        root((0,), 1)
+        root((1,), 1)
+        square((0,), 1)
+        square((1,), 1)
         root((2,), 1)
+        square((2,), 0)
         square((2,), 1)
         root((3,), 1)
+        square((3,), 0)
         square((3,), 1)
         sign((0, 1), 0)
+        sign((2, 3), 0)
+        square_v((0, 1), 0)
         sign((0, 1), 1)
         recip(0)
         recip(1)
-        sign((2, 3), 0)
-        assign(0, True, 1)
         sign((2, 3), 1)
         recip(2)
+        assign(0, False, 1)
         assign(1, True, 1)
         recip(3)
         assign(2, False, 1)

@@ -18,12 +18,16 @@ ACT = mybir.ActivationFunctionType
 AX = mybir.AxisListType
 
 P = 128
+QUAD = 32
 PACK = 4
+LIST_ROWS = 16
 TILES = I // P
 BLOCKS = M // P
 HALF = M // 2
-SPLIT = 192
+RUN = 4
+CAST_SPLIT = 192
 TINY = 2.0**-60
+ROW_TOTAL = 512.0
 
 
 def tile_attend_dectarget_kernel(tc, pts_words, pts_scales, cent, pn, cn, offs, out):
@@ -32,25 +36,27 @@ def tile_attend_dectarget_kernel(tc, pts_words, pts_scales, cent, pn, cn, offs, 
         sb = ctx.enter_context(tc.tile_pool(name="sb", bufs=1))
         ps = ctx.enter_context(tc.psum_pool(name="ps", bufs=1))
 
-        offsets = sb.tile([P, I // 16], U16, name="offsets")
+        offsets = sb.tile([P, I // LIST_ROWS], U16, name="offsets")
         words = sb.tile([P, T], U16, name="words", align_bytes=64)
-        plane = sb.tile([P, T], U8, name="plane", align_bytes=64)
+        scale_pool = sb.tile([P, T], U8, name="scale_pool", align_bytes=64)
         raw = [sb.tile([P, PACK, HALF], F32, name="raw%d" % h) for h in range(2)]
         pn_col = sb.tile([P, TILES], F32, name="pn_col")
         cn_col = sb.tile([P, BLOCKS], F32, name="cn_col")
         ident = sb.tile([P, P], F32, name="ident")
 
-        nc.vector.memset(plane[:].bitcast(I32), 0)
-        ones = sb.tile([P, 32], F32, name="ones")
-        ramp = sb.tile([P, 32], F32, name="ramp", align_bytes=64)
-        lane = sb.tile([P, 32], F32, name="lane", align_bytes=64)
+        nc.vector.memset(scale_pool[:].bitcast(I32), 0)
+
+        ones = sb.tile([P, QUAD], F32, name="ones")
+        ramp = sb.tile([P, QUAD], F32, name="ramp", align_bytes=64)
+        lane = sb.tile([P, QUAD], F32, name="lane", align_bytes=64)
         nc.vector.memset(ones[:], 1.0)
         nc.vector.memset(ident[:], 0.0)
         nc.vector.tensor_tensor_scan(ramp[:], ones[:], ones[:], -1.0, ALU.mult, ALU.add)
         nc.vector.transpose(lane[:], ramp[:])
-        for c in range(4):
-            rows = slice(32 * c, 32 * c + 32)
+        for quad in range(P // QUAD):
+            rows = slice(QUAD * quad, QUAD * (quad + 1))
             nc.vector.tensor_tensor(ident[rows, rows], ramp[rows, :], lane[rows, :], ALU.is_equal)
+
         warm = sb.tile([P, 1], F32, name="warm")
         nc.scalar.activation(out=warm[:], in_=ones[:, 0:1], func=ACT.Abs_reciprocal_sqrt)
 
@@ -58,42 +64,47 @@ def tile_attend_dectarget_kernel(tc, pts_words, pts_scales, cent, pn, cn, offs, 
         nc.sync.dma_start(offsets[:], offs)
         nc.sync.dma_start(raw[0][:], cent_rows[:, :, 0:HALF])
         nc.sync.dma_start(cn_col[:], cn.rearrange("o (p b) -> p (o b)", p=P))
-        for q in range(4):
+        for quad in range(P // QUAD):
             nc.sync.dma_start(
-                plane[32 * q : 32 * q + 4, :].bitcast(I32),
-                pts_scales[0, 4 * q : 4 * q + 4, :].bitcast(I32),
+                scale_pool[QUAD * quad : QUAD * quad + PACK, :].bitcast(I32),
+                pts_scales[0, PACK * quad : PACK * (quad + 1), :].bitcast(I32),
             )
         nc.sync.dma_start(words[:].bitcast(I32), pts_words[0].bitcast(I32))
         nc.sync.dma_start(raw[1][:], cent_rows[:, :, HALF:M])
-        with nc.allow_non_contiguous_dma(reason="one number a partition"):
+        with nc.allow_non_contiguous_dma(reason="one number for each partition and row tile"):
             nc.gpsimd.dma_start(pn_col[:], pn.rearrange("(t p) o -> p (t o)", p=P))
 
-        row_ps = ps.tile([P, M], F32, name="row_ps")
+        cn_ps = ps.tile([P, M], F32, name="row_bank")
         for b in range(BLOCKS):
-            nc.tensor.transpose(row_ps[:, b * P : (b + 1) * P], cn_col[:, b : b + 1].to_broadcast([P, P]), ident[:])
-        cn1 = sb.tile([P, M], F32, name="cn1")
+            nc.tensor.transpose(cn_ps[:, b * P : (b + 1) * P], cn_col[:, b : b + 1].to_broadcast([P, P]), ident[:])
+        cn_plus_1 = sb.tile([P, M], F32, name="cn_plus_1")
 
-        cscale = [sb.tile([P, HALF], U8, name="cscale%d" % h, align_bytes=64) for h in range(2)]
-        gs = sb.tile([P, I], U8, name="gs", align_bytes=64)
+        cent_scales = [sb.tile([P, HALF], U8, name="cent_scales%d" % h, align_bytes=64) for h in range(2)]
+        pts_scale = sb.tile([P, I], U8, name="pts_scale", align_bytes=64)
         grouped = [sb.tile([P, HALF, PACK], BF16, name="grouped%d" % h, align_bytes=64) for h in range(2)]
 
-        def cast(h, lo, hi, on_vector):
-            dst = grouped[h][:, lo:hi, :].rearrange("p (c i) j -> p c j i", i=4)
-            src = raw[h][:, :, lo:hi].rearrange("p j (c i) -> p c j i", i=4)
-            if on_vector:
-                nc.vector.tensor_scalar(out=dst, in0=src, scalar1=-2.0, scalar2=None, op0=ALU.mult)
-            else:
-                nc.scalar.activation(out=dst, in_=src, func=ACT.Copy, scale=-2.0)
+        def cast_views(h, lo, hi):
+            dst = grouped[h][:, lo:hi, :].rearrange("p (c n) j -> p c j n", n=RUN)
+            src = raw[h][:, :, lo:hi].rearrange("p j (c n) -> p c j n", n=RUN)
+            return dst, src
 
-        def quant(h):
+        def cast_on_scalar(h, lo, hi):
+            dst, src = cast_views(h, lo, hi)
+            nc.scalar.activation(out=dst, in_=src, func=ACT.Copy, scale=-2.0)
+
+        def cast_on_vector(h, lo, hi):
+            dst, src = cast_views(h, lo, hi)
+            nc.vector.tensor_scalar(out=dst, in0=src, scalar1=-2.0, scalar2=None, op0=ALU.mult)
+
+        def quantise(h):
             nc.vector.quantize_mx(
-                out=codes[h][:].bitcast(FP8X4),
-                scales=cscale[h][:],
-                in_=grouped[h][:].rearrange("p w j -> p (w j)"),
+                out=cent_codes[h][:].bitcast(FP8X4),
+                scales=cent_scales[h][:],
+                in_=grouped[h][:].rearrange("p m j -> p (m j)"),
             )
 
         def paired(name):
-            return [sb.tile([P, 2, 2, HALF], F32, name="%s%d" % (name, c)) for c in range(2)]
+            return [sb.tile([P, 2, 2, HALF], F32, name="%s%d" % (name, pair)) for pair in range(TILES // 2)]
 
         def wide(name):
             return [sb.tile([P, M], F32, name="%s%d" % (name, t)) for t in range(TILES)]
@@ -101,158 +112,188 @@ def tile_attend_dectarget_kernel(tc, pts_words, pts_scales, cent, pn, cn, offs, 
         def narrow(name):
             return [sb.tile([P, 1], F32, name="%s%d" % (name, t)) for t in range(TILES)]
 
-        u, v, g = [paired(n) for n in ("u", "v", "g")]
-        x = []
-        q, r, s, y, res = [wide(n) for n in ("q", "r", "s", "y", "res")]
-        rs, ir, ys, iy, k = [narrow(n) for n in ("rs", "ir", "ys", "iy", "k")]
-        colsum = []
+        def part(values, tiles, h):
+            return values[tiles[0] // 2][:, h, tiles[0] % 2 : tiles[-1] % 2 + 1, :]
 
-        def score(tiles, h):
-            name = "row_ps" if (tiles[0], h) == (0, 0) else "a_ps%d%d" % (tiles[0], h)
-            a_ps = ps.tile([P, 2, HALF], F32, name=name)
+        inv_root, inv_abs, clamped = [paired(n) for n in ("inv_root", "inv_abs", "clamped")]
+        s_sq, signed, s, y, result = [wide(n) for n in ("s_sq", "signed", "s", "y", "result")]
+        signed_sum, inv_signed_sum, y_sum, inv_y_sum = [
+            narrow(n) for n in ("signed_sum", "inv_signed_sum", "y_sum", "inv_y_sum")
+        ]
+
+        def denominators(tiles, h, bank):
+            scores = ps.tile([P, 2, HALF], F32, name=bank)
             for e, t in enumerate(tiles):
                 nc.tensor.matmul_mx(
-                    out=a_ps[:, e, :],
-                    lhsT=gw[t // 2][:, (t % 2) * P : (t % 2 + 1) * P].bitcast(FP4X4),
-                    lhsT_scale=gs[:, t * P : (t + 1) * P],
-                    rhs=codes[h][:].bitcast(FP8X4),
-                    rhs_scale=cscale[h][:],
+                    out=scores[:, e, :],
+                    lhsT=pts_codes[t // 2][:, (t % 2) * P : (t % 2 + 1) * P].bitcast(FP4X4),
+                    lhsT_scale=pts_scale[:, t * P : (t + 1) * P],
+                    rhs=cent_codes[h][:].bitcast(FP8X4),
+                    rhs_scale=cent_scales[h][:],
                     start=True,
                     stop=True,
                 )
             for e, t in enumerate(tiles):
                 nc.vector.scalar_tensor_tensor(
-                    out=x[t // 2][:, h, t % 2, :],
-                    in0=a_ps[:, e, :],
+                    out=den[t // 2][:, h, t % 2, :],
+                    in0=scores[:, e, :],
                     scalar=pn_col[:, t : t + 1],
-                    in1=cn1[:, h * HALF : (h + 1) * HALF],
+                    in1=cn_plus_1[:, h * HALF : (h + 1) * HALF],
                     op0=ALU.add,
                     op1=ALU.add,
                 )
 
-        def part(arr, tiles, h):
-            c = tiles[0] // 2
-            return arr[c][:, h, tiles[0] % 2 : tiles[-1] % 2 + 1, :]
-
-        def square_v(tiles, h):
-            nc.vector.tensor_tensor(part(v, tiles, h), part(u, tiles, h), part(u, tiles, h), ALU.mult)
-
         def root(tiles, h):
-            nc.scalar.activation(out=part(u, tiles, h), in_=part(x, tiles, h), func=ACT.Abs_reciprocal_sqrt)
+            nc.scalar.activation(out=part(inv_root, tiles, h), in_=part(den, tiles, h), func=ACT.Abs_reciprocal_sqrt)
 
-        def square(tiles, h):
-            nc.scalar.activation(out=part(v, tiles, h), in_=part(u, tiles, h), func=ACT.Square)
+        def square_on_scalar(tiles, h):
+            nc.scalar.activation(out=part(inv_abs, tiles, h), in_=part(inv_root, tiles, h), func=ACT.Square)
 
-        def sign(tiles, h):
-            engine = nc.gpsimd if h == 0 else nc.vector
+        def square_on_vector(tiles, h):
+            nc.vector.tensor_tensor(part(inv_abs, tiles, h), part(inv_root, tiles, h), part(inv_root, tiles, h), ALU.mult)
+
+        def clamp(engine, tiles, h):
             engine.tensor_scalar(
-                out=part(g, tiles, h), in0=part(x, tiles, h), scalar1=TINY, scalar2=-TINY, op0=ALU.min, op1=ALU.max
+                out=part(clamped, tiles, h),
+                in0=part(den, tiles, h),
+                scalar1=TINY,
+                scalar2=-TINY,
+                op0=ALU.min,
+                op1=ALU.max,
             )
 
-        def recip(t):
+        def signed_and_row_sum(t):
             nc.vector.scalar_tensor_tensor(
-                out=r[t][:].rearrange("p (h w) -> p h w", h=2),
-                in0=g[t // 2][:, :, t % 2, :],
+                out=signed[t][:].rearrange("p (h m) -> p h m", h=2),
+                in0=clamped[t // 2][:, :, t % 2, :],
                 scalar=1.0,
-                in1=v[t // 2][:, :, t % 2, :],
+                in1=inv_abs[t // 2][:, :, t % 2, :],
                 op0=ALU.mult,
                 op1=ALU.mult,
-                accum_out=rs[t][:],
+                accum_out=signed_sum[t][:],
             )
-            nc.vector.reciprocal(ir[t][:], rs[t][:])
+            nc.vector.reciprocal(inv_signed_sum[t][:], signed_sum[t][:])
 
-        def assign(t, on_vector, halves):
-            for h in range(halves):
-                cols = slice(h * M // halves, (h + 1) * M // halves)
-                if on_vector:
-                    nc.vector.tensor_scalar(out=s[t][:, cols], in0=r[t][:, cols], scalar1=ir[t][:], scalar2=None, op0=ALU.mult)
-                else:
-                    nc.scalar.activation(out=s[t][:, cols], in_=r[t][:, cols], func=ACT.Copy, scale=ir[t][:])
-            for b in range(BLOCKS):
-                if t == 0:
-                    colsum.append(ps.tile([P, P], F32, name=("a_ps10", "a_ps20", "sum2", "sum3")[b]))
+        def s_on_vector(t):
+            nc.vector.tensor_scalar(
+                out=s[t][:], in0=signed[t][:], scalar1=inv_signed_sum[t][:], scalar2=None, op0=ALU.mult
+            )
+
+        def s_on_scalar(t):
+            nc.scalar.activation(out=s[t][:], in_=signed[t][:], func=ACT.Copy, scale=inv_signed_sum[t][:])
+
+        col_parts = []
+
+        def add_to_column_sums(source, first, last):
+            for b, bank in enumerate(("bank_1_0", "bank_23_0", "bank_sum2", "bank_sum3")):
+                if first:
+                    col_parts.append(ps.tile([P, P], F32, name=bank))
                 nc.tensor.matmul(
-                    colsum[b][:],
-                    lhsT=s[t][:, b * P : (b + 1) * P],
+                    col_parts[b][:],
+                    lhsT=source[:, b * P : (b + 1) * P],
                     rhs=ident[:],
                     is_transpose=True,
-                    start=(t == 0),
-                    stop=(t == TILES - 1),
+                    start=first,
+                    stop=last,
                 )
 
-        cast(0, 0, HALF, False)
+        cast_on_scalar(0, 0, HALF)
         nc.scalar.activation(
-            out=cn1[:].rearrange("p (n b) -> p n b", b=BLOCKS),
-            in_=row_ps[:].rearrange("p (b n) -> p n b", b=BLOCKS),
+            out=cn_plus_1[:].rearrange("p (n b) -> p n b", b=BLOCKS),
+            in_=cn_ps[:].rearrange("p (b n) -> p n b", b=BLOCKS),
             func=ACT.Copy,
             bias=1.0,
         )
-        cast(1, 0, SPLIT, False)
-        nc.vector.tensor_copy(gs[:], plane[:].indirect(offsets[:]))
-        codes = [sb.tile([P, HALF], U32, name=n, align_bytes=64) for n in ("plane", "codes1")]
-        quant(0)
-        gw = [sb.tile([P, I // 2], U16, name=n, align_bytes=64) for n in ("gw0", "gw1")]
+        cast_on_scalar(1, 0, CAST_SPLIT)
+        nc.vector.tensor_copy(pts_scale[:], scale_pool[:].indirect(offsets[:]))
+        cent_codes = [sb.tile([P, HALF], U32, name=n, align_bytes=64) for n in ("scale_pool", "cent_codes1")]
+        quantise(0)
+        pts_codes = [sb.tile([P, 2 * P], U16, name="pts_codes%d" % pair, align_bytes=64) for pair in range(TILES // 2)]
+        pair_columns = 2 * P // LIST_ROWS
+        for pair in range(TILES // 2):
+            entries = offsets[:, pair_columns * pair : pair_columns * (pair + 1)]
+            nc.vector.tensor_copy(pts_codes[pair][:], words[:].indirect(entries))
+        cast_on_vector(1, CAST_SPLIT, HALF)
+        quantise(1)
+
+        den_all = sb.tile([P, 2, 2, 2, HALF], F32, name="grouped1", align_bytes=64)
+        den = [den_all[:, pair] for pair in range(TILES // 2)]
         for h in range(2):
-            nc.vector.tensor_copy(gw[h][:], words[:].indirect(offsets[:, 16 * h : 16 * h + 16]))
-        cast(1, SPLIT, HALF, True)
-        quant(1)
-        x_all = sb.tile([P, 2, 2, 2, HALF], F32, name="grouped1", align_bytes=64)
-        x.extend([x_all[:, 0], x_all[:, 1]])
-        score((0,), 0)
-        score((1,), 0)
-        score((2, 3), 0)
-        score((0,), 1)
-        score((1,), 1)
-        score((2, 3), 1)
+            denominators((0,), h, "row_bank" if h == 0 else "bank_0_1")
+            denominators((1,), h, "bank_1_%d" % h)
+            denominators((2, 3), h, "bank_23_%d" % h)
+
         root((0, 1), 0)
         root((2, 3), 0)
         root((0,), 1)
         root((1,), 1)
-        square((0,), 1)
-        square((1,), 1)
-        root((2,), 1)
-        square((2,), 0)
-        square((2,), 1)
-        root((3,), 1)
-        square((3,), 0)
-        square((3,), 1)
-        sign((0, 1), 0)
-        sign((2, 3), 0)
-        square_v((0, 1), 0)
-        sign((0, 1), 1)
-        recip(0)
-        recip(1)
-        sign((2, 3), 1)
-        recip(2)
-        assign(0, False, 1)
-        assign(1, True, 1)
-        recip(3)
-        assign(2, False, 1)
-        assign(3, True, 2)
-        for t in range(TILES):
-            nc.scalar.activation(out=q[t][:], in_=r[t][:], func=ACT.Square, scale=ir[t][:])
+        square_on_scalar((0,), 1)
+        for t in range(1, TILES):
+            if t > 1:
+                root((t,), 1)
+            square_on_scalar((t,), 0)
+            square_on_scalar((t,), 1)
 
-        w_ps = ps.tile([P, M], F32, name="row_ps")
+        clamp(nc.gpsimd, (0, 1), 0)
+        clamp(nc.gpsimd, (2, 3), 0)
+        square_on_vector((0,), 0)
+        clamp(nc.vector, (0, 1), 1)
+        clamp(nc.vector, (2, 3), 1)
+
+        for t in range(TILES - 1):
+            signed_and_row_sum(t)
+        s_on_vector(1)
+        add_to_column_sums(s[1], first=True, last=False)
+        s_on_scalar(0)
+        add_to_column_sums(s[0], first=False, last=False)
+        signed_and_row_sum(3)
+        s_on_scalar(2)
+        s_2_plus_3 = s[3]
+        for h in range(2):
+            cols = slice(h * HALF, (h + 1) * HALF)
+            nc.vector.scalar_tensor_tensor(
+                out=s_2_plus_3[:, cols],
+                in0=signed[3][:, cols],
+                scalar=inv_signed_sum[3][:],
+                in1=s[2][:, cols],
+                op0=ALU.mult,
+                op1=ALU.add,
+            )
+        add_to_column_sums(s_2_plus_3, first=False, last=True)
+
+        for t in range(TILES):
+            nc.scalar.activation(out=s_sq[t][:], in_=signed[t][:], func=ACT.Square, scale=inv_signed_sum[t][:])
+
+        w_ps = ps.tile([P, M], F32, name="row_bank")
         for b in range(BLOCKS):
-            ssum = sb.tile([P, 1], F32, name="ssum%d" % b)
-            nc.vector.tensor_reduce(out=ssum[:], in_=colsum[b][:], axis=AX.X, op=ALU.add)
-            w = sb.tile([P, 1], F32, name="w%d" % b)
-            nc.vector.reciprocal(w[:], ssum[:])
-            nc.tensor.transpose(w_ps[:, b * P : (b + 1) * P], w[:].to_broadcast([P, P]), ident[:])
+            col_sum = sb.tile([P, 1], F32, name="col_sum%d" % b)
+            nc.vector.tensor_reduce(out=col_sum[:], in_=col_parts[b][:], axis=AX.X, op=ALU.add)
+            w_col = sb.tile([P, 1], F32, name="w_col%d" % b)
+            nc.vector.reciprocal(w_col[:], col_sum[:])
+            nc.tensor.transpose(w_ps[:, b * P : (b + 1) * P], w_col[:].to_broadcast([P, P]), ident[:])
 
         for t in range(TILES):
             nc.vector.scalar_tensor_tensor(
-                out=y[t][:], in0=q[t][:], scalar=1.0, in1=w_ps[:], op0=ALU.mult, op1=ALU.mult, accum_out=ys[t][:]
+                out=y[t][:],
+                in0=s_sq[t][:],
+                scalar=1.0,
+                in1=w_ps[:],
+                op0=ALU.mult,
+                op1=ALU.mult,
+                accum_out=y_sum[t][:],
             )
-            nc.vector.reciprocal(iy[t][:], ys[t][:])
+            nc.vector.reciprocal(inv_y_sum[t][:], y_sum[t][:])
             if t == 0:
-                nc.scalar.activation(out=k[t][:], in_=iy[t][:], func=ACT.Copy, scale=512.0)
-            for h in range(1):
-                cols = slice(h * M // 1, (h + 1) * M // 1)
-                if t > 0:
-                    nc.vector.tensor_scalar(
-                        out=res[t][:, cols], in0=y[t][:, cols], scalar1=iy[t][:], scalar2=512.0, op0=ALU.mult, op1=ALU.mult
-                    )
-                else:
-                    nc.scalar.activation(out=res[t][:, cols], in_=y[t][:, cols], func=ACT.Copy, scale=k[t][:])
-                nc.sync.dma_start(out[t * P : (t + 1) * P, cols], res[t][:, cols])
+                row_scale = sb.tile([P, 1], F32, name="row_scale")
+                nc.scalar.activation(out=row_scale[:], in_=inv_y_sum[t][:], func=ACT.Copy, scale=ROW_TOTAL)
+                nc.scalar.activation(out=result[t][:], in_=y[t][:], func=ACT.Copy, scale=row_scale[:])
+            else:
+                nc.vector.tensor_scalar(
+                    out=result[t][:],
+                    in0=y[t][:],
+                    scalar1=inv_y_sum[t][:],
+                    scalar2=ROW_TOTAL,
+                    op0=ALU.mult,
+                    op1=ALU.mult,
+                )
+            nc.sync.dma_start(out[t * P : (t + 1) * P, :], result[t][:])

from contextlib import ExitStack

import concourse.mybir as mybir

D, T, I, M = 512, 2048, 512, 512
FLOPS = 2 * D * I * M

F32 = mybir.dt.float32
BF16 = mybir.dt.bfloat16
I32 = mybir.dt.int32
U32 = mybir.dt.uint32
U16 = mybir.dt.uint16
U8 = mybir.dt.uint8
FP8X4 = mybir.dt.float8_e4m3fn_x4
FP4X4 = mybir.dt.float4_e2m1fn_x4
ALU = mybir.AluOpType
ACT = mybir.ActivationFunctionType
AX = mybir.AxisListType

P = 128
QUAD = 32
PACK = 4
LIST_ROWS = 16
TILES = I // P
BLOCKS = M // P
HALF = M // 2
RUN = 4
CAST_SPLIT = 192
TINY = 2.0**-60
ROW_TOTAL = 512.0


def tile_attend_dectarget_kernel(tc, pts_words, pts_scales, cent, pn, cn, offs, out):
    nc = tc.nc
    with ExitStack() as ctx:
        sb = ctx.enter_context(tc.tile_pool(name="sb", bufs=1))
        ps = ctx.enter_context(tc.psum_pool(name="ps", bufs=1))

        offsets = sb.tile([P, I // LIST_ROWS], U16, name="offsets")
        words = sb.tile([P, T], U16, name="words", align_bytes=64)
        scale_pool = sb.tile([P, T], U8, name="scale_pool", align_bytes=64)
        raw = [sb.tile([P, PACK, HALF], F32, name="raw%d" % h) for h in range(2)]
        pn_col = sb.tile([P, TILES], F32, name="pn_col")
        cn_col = sb.tile([P, BLOCKS], F32, name="cn_col")
        ident = sb.tile([P, P], F32, name="ident")

        nc.vector.memset(scale_pool[:].bitcast(I32), 0)

        ones = sb.tile([P, QUAD], F32, name="ones")
        ramp = sb.tile([P, QUAD], F32, name="ramp", align_bytes=64)
        lane = sb.tile([P, QUAD], F32, name="lane", align_bytes=64)
        nc.vector.memset(ones[:], 1.0)
        nc.vector.memset(ident[:], 0.0)
        nc.vector.tensor_tensor_scan(ramp[:], ones[:], ones[:], -1.0, ALU.mult, ALU.add)
        nc.vector.transpose(lane[:], ramp[:])
        for quad in range(P // QUAD):
            rows = slice(QUAD * quad, QUAD * (quad + 1))
            nc.vector.tensor_tensor(ident[rows, rows], ramp[rows, :], lane[rows, :], ALU.is_equal)

        warm = sb.tile([P, 1], F32, name="warm")
        nc.scalar.activation(out=warm[:], in_=ones[:, 0:1], func=ACT.Abs_reciprocal_sqrt)

        cent_rows = cent.rearrange("(p j) m -> p j m", j=PACK)
        nc.sync.dma_start(offsets[:], offs)
        nc.sync.dma_start(raw[0][:], cent_rows[:, :, 0:HALF])
        nc.sync.dma_start(cn_col[:], cn.rearrange("o (p b) -> p (o b)", p=P))
        for quad in range(P // QUAD):
            nc.sync.dma_start(
                scale_pool[QUAD * quad : QUAD * quad + PACK, :].bitcast(I32),
                pts_scales[0, PACK * quad : PACK * (quad + 1), :].bitcast(I32),
            )
        nc.sync.dma_start(words[:].bitcast(I32), pts_words[0].bitcast(I32))
        nc.sync.dma_start(raw[1][:], cent_rows[:, :, HALF:M])
        with nc.allow_non_contiguous_dma(reason="one number for each partition and row tile"):
            nc.gpsimd.dma_start(pn_col[:], pn.rearrange("(t p) o -> p (t o)", p=P))

        cn_ps = ps.tile([P, M], F32, name="row_bank")
        for b in range(BLOCKS):
            nc.tensor.transpose(cn_ps[:, b * P : (b + 1) * P], cn_col[:, b : b + 1].to_broadcast([P, P]), ident[:])
        cn_plus_1 = sb.tile([P, M], F32, name="cn_plus_1")

        cent_scales = [sb.tile([P, HALF], U8, name="cent_scales%d" % h, align_bytes=64) for h in range(2)]
        pts_scale = sb.tile([P, I], U8, name="pts_scale", align_bytes=64)
        grouped = [sb.tile([P, HALF, PACK], BF16, name="grouped%d" % h, align_bytes=64) for h in range(2)]

        def cast_views(h, lo, hi):
            dst = grouped[h][:, lo:hi, :].rearrange("p (c n) j -> p c j n", n=RUN)
            src = raw[h][:, :, lo:hi].rearrange("p j (c n) -> p c j n", n=RUN)
            return dst, src

        def cast_on_scalar(h, lo, hi):
            dst, src = cast_views(h, lo, hi)
            nc.scalar.activation(out=dst, in_=src, func=ACT.Copy, scale=-2.0)

        def cast_on_vector(h, lo, hi):
            dst, src = cast_views(h, lo, hi)
            nc.vector.tensor_scalar(out=dst, in0=src, scalar1=-2.0, scalar2=None, op0=ALU.mult)

        def quantise(h):
            nc.vector.quantize_mx(
                out=cent_codes[h][:].bitcast(FP8X4),
                scales=cent_scales[h][:],
                in_=grouped[h][:].rearrange("p m j -> p (m j)"),
            )

        def paired(name):
            return [sb.tile([P, 2, 2, HALF], F32, name="%s%d" % (name, pair)) for pair in range(TILES // 2)]

        def wide(name):
            return [sb.tile([P, M], F32, name="%s%d" % (name, t)) for t in range(TILES)]

        def narrow(name):
            return [sb.tile([P, 1], F32, name="%s%d" % (name, t)) for t in range(TILES)]

        def part(values, tiles, h):
            return values[tiles[0] // 2][:, h, tiles[0] % 2 : tiles[-1] % 2 + 1, :]

        inv_root, inv_abs, clamped = [paired(n) for n in ("inv_root", "inv_abs", "clamped")]
        s_sq, signed, s, y, result = [wide(n) for n in ("s_sq", "signed", "s", "y", "result")]
        signed_sum, inv_signed_sum, y_sum, inv_y_sum = [
            narrow(n) for n in ("signed_sum", "inv_signed_sum", "y_sum", "inv_y_sum")
        ]

        def denominators(tiles, h, bank):
            scores = ps.tile([P, 2, HALF], F32, name=bank)
            for e, t in enumerate(tiles):
                nc.tensor.matmul_mx(
                    out=scores[:, e, :],
                    lhsT=pts_codes[t // 2][:, (t % 2) * P : (t % 2 + 1) * P].bitcast(FP4X4),
                    lhsT_scale=pts_scale[:, t * P : (t + 1) * P],
                    rhs=cent_codes[h][:].bitcast(FP8X4),
                    rhs_scale=cent_scales[h][:],
                    start=True,
                    stop=True,
                )
            for e, t in enumerate(tiles):
                nc.vector.scalar_tensor_tensor(
                    out=den[t // 2][:, h, t % 2, :],
                    in0=scores[:, e, :],
                    scalar=pn_col[:, t : t + 1],
                    in1=cn_plus_1[:, h * HALF : (h + 1) * HALF],
                    op0=ALU.add,
                    op1=ALU.add,
                )

        def root(tiles, h):
            nc.scalar.activation(out=part(inv_root, tiles, h), in_=part(den, tiles, h), func=ACT.Abs_reciprocal_sqrt)

        def square_on_scalar(tiles, h):
            nc.scalar.activation(out=part(inv_abs, tiles, h), in_=part(inv_root, tiles, h), func=ACT.Square)

        def square_on_vector(tiles, h):
            nc.vector.tensor_tensor(part(inv_abs, tiles, h), part(inv_root, tiles, h), part(inv_root, tiles, h), ALU.mult)

        def clamp(engine, tiles, h):
            engine.tensor_scalar(
                out=part(clamped, tiles, h),
                in0=part(den, tiles, h),
                scalar1=TINY,
                scalar2=-TINY,
                op0=ALU.min,
                op1=ALU.max,
            )

        def signed_and_row_sum(t):
            nc.vector.scalar_tensor_tensor(
                out=signed[t][:].rearrange("p (h m) -> p h m", h=2),
                in0=clamped[t // 2][:, :, t % 2, :],
                scalar=1.0,
                in1=inv_abs[t // 2][:, :, t % 2, :],
                op0=ALU.mult,
                op1=ALU.mult,
                accum_out=signed_sum[t][:],
            )
            nc.vector.reciprocal(inv_signed_sum[t][:], signed_sum[t][:])

        def s_on_vector(t):
            nc.vector.tensor_scalar(
                out=s[t][:], in0=signed[t][:], scalar1=inv_signed_sum[t][:], scalar2=None, op0=ALU.mult
            )

        def s_on_scalar(t):
            nc.scalar.activation(out=s[t][:], in_=signed[t][:], func=ACT.Copy, scale=inv_signed_sum[t][:])

        col_parts = []

        def add_to_column_sums(source, first, last):
            for b, bank in enumerate(("bank_1_0", "bank_23_0", "bank_sum2", "bank_sum3")):
                if first:
                    col_parts.append(ps.tile([P, P], F32, name=bank))
                nc.tensor.matmul(
                    col_parts[b][:],
                    lhsT=source[:, b * P : (b + 1) * P],
                    rhs=ident[:],
                    is_transpose=True,
                    start=first,
                    stop=last,
                )

        cast_on_scalar(0, 0, HALF)
        nc.scalar.activation(
            out=cn_plus_1[:].rearrange("p (n b) -> p n b", b=BLOCKS),
            in_=cn_ps[:].rearrange("p (b n) -> p n b", b=BLOCKS),
            func=ACT.Copy,
            bias=1.0,
        )
        cast_on_scalar(1, 0, CAST_SPLIT)
        nc.vector.tensor_copy(pts_scale[:], scale_pool[:].indirect(offsets[:]))
        cent_codes = [sb.tile([P, HALF], U32, name=n, align_bytes=64) for n in ("scale_pool", "cent_codes1")]
        quantise(0)
        pts_codes = [sb.tile([P, 2 * P], U16, name="pts_codes%d" % pair, align_bytes=64) for pair in range(TILES // 2)]
        pair_columns = 2 * P // LIST_ROWS
        for pair in range(TILES // 2):
            entries = offsets[:, pair_columns * pair : pair_columns * (pair + 1)]
            nc.vector.tensor_copy(pts_codes[pair][:], words[:].indirect(entries))
        cast_on_vector(1, CAST_SPLIT, HALF)
        quantise(1)

        den_all = sb.tile([P, 2, 2, 2, HALF], F32, name="grouped1", align_bytes=64)
        den = [den_all[:, pair] for pair in range(TILES // 2)]
        for h in range(2):
            denominators((0,), h, "row_bank" if h == 0 else "bank_0_1")
            denominators((1,), h, "bank_1_%d" % h)
            denominators((2, 3), h, "bank_23_%d" % h)

        root((0, 1), 0)
        root((2, 3), 0)
        root((0,), 1)
        root((1,), 1)
        square_on_scalar((0,), 1)
        for t in range(1, TILES):
            if t > 1:
                root((t,), 1)
            square_on_scalar((t,), 0)
            square_on_scalar((t,), 1)

        clamp(nc.gpsimd, (0, 1), 0)
        clamp(nc.gpsimd, (2, 3), 0)
        square_on_vector((0,), 0)
        clamp(nc.vector, (0, 1), 1)
        clamp(nc.vector, (2, 3), 1)

        for t in range(TILES - 1):
            signed_and_row_sum(t)
        s_on_vector(1)
        add_to_column_sums(s[1], first=True, last=False)
        s_on_scalar(0)
        add_to_column_sums(s[0], first=False, last=False)
        signed_and_row_sum(3)
        s_on_scalar(2)
        s_2_plus_3 = s[3]
        for h in range(2):
            cols = slice(h * HALF, (h + 1) * HALF)
            nc.vector.scalar_tensor_tensor(
                out=s_2_plus_3[:, cols],
                in0=signed[3][:, cols],
                scalar=inv_signed_sum[3][:],
                in1=s[2][:, cols],
                op0=ALU.mult,
                op1=ALU.add,
            )
        add_to_column_sums(s_2_plus_3, first=False, last=True)

        for t in range(TILES):
            nc.scalar.activation(out=s_sq[t][:], in_=signed[t][:], func=ACT.Square, scale=inv_signed_sum[t][:])

        w_ps = ps.tile([P, M], F32, name="row_bank")
        for b in range(BLOCKS):
            col_sum = sb.tile([P, 1], F32, name="col_sum%d" % b)
            nc.vector.tensor_reduce(out=col_sum[:], in_=col_parts[b][:], axis=AX.X, op=ALU.add)
            w_col = sb.tile([P, 1], F32, name="w_col%d" % b)
            nc.vector.reciprocal(w_col[:], col_sum[:])
            nc.tensor.transpose(w_ps[:, b * P : (b + 1) * P], w_col[:].to_broadcast([P, P]), ident[:])

        for t in range(TILES):
            nc.vector.scalar_tensor_tensor(
                out=y[t][:],
                in0=s_sq[t][:],
                scalar=1.0,
                in1=w_ps[:],
                op0=ALU.mult,
                op1=ALU.mult,
                accum_out=y_sum[t][:],
            )
            nc.vector.reciprocal(inv_y_sum[t][:], y_sum[t][:])
            if t == 0:
                row_scale = sb.tile([P, 1], F32, name="row_scale")
                nc.scalar.activation(out=row_scale[:], in_=inv_y_sum[t][:], func=ACT.Copy, scale=ROW_TOTAL)
                nc.scalar.activation(out=result[t][:], in_=y[t][:], func=ACT.Copy, scale=row_scale[:])
            else:
                nc.vector.tensor_scalar(
                    out=result[t][:],
                    in0=y[t][:],
                    scalar1=inv_y_sum[t][:],
                    scalar2=ROW_TOTAL,
                    op0=ALU.mult,
                    op1=ALU.mult,
                )
            nc.sync.dma_start(out[t * P : (t + 1) * P, :], result[t][:])
